import numpy as np
import ml_dtypes


def mxq(x, axis, fmt="e4m3"):
    dtype, down = {"e4m3": (ml_dtypes.float8_e4m3fn, 7), "e5m2": (ml_dtypes.float8_e5m2, 14)}[fmt]
    v = np.moveaxis(np.asarray(x, np.float32).astype(ml_dtypes.bfloat16).astype(np.float64), axis, -1)
    blocks = v.reshape(v.shape[:-1] + (-1, 32))
    amax = np.abs(blocks).max(-1, keepdims=True)
    byte = np.maximum(np.where(amax > 0, np.frexp(amax)[1] - 1 + 127, 0) - down, 1)
    scale = np.exp2(byte - 127.0)
    codes = (blocks / scale).astype(np.float32).astype(dtype).astype(np.float64)
    return np.moveaxis((codes * scale).reshape(v.shape), -1, axis)


WIDE = False


def mx_kscale(k):
    if not WIDE:
        return np.ones(k)
    levels = np.array([10, -10, 5, -5, 0])
    if k % 512:
        return np.exp2(np.random.permutation(np.resize(levels, k // 32))).repeat(32)
    a = np.empty((k // 512, 16))
    for p in range(k // 512):
        a[p, :8] = np.random.permutation(np.resize(levels, 8))
        for g in range(8):
            far = levels[np.abs(levels - a[p, g]) >= 10]
            a[p, g + 8] = far[np.random.randint(len(far))]
    return np.exp2(a.ravel()).repeat(32)


def f64(x):
    return np.asarray(x).astype(np.float64)


def striped(idx):
    return np.tile(idx.reshape(-1, 16).T, (8, 1)).astype(np.uint16)


def unstriped(offs):
    return offs[:16].T.reshape(-1).astype(np.int64)


def striped8(idx):
    return np.concatenate([x.reshape(-1, 16).T for x in idx]).astype(np.uint16)


def runs(offs, k):
    lists = np.stack([offs[16 * r : 16 * r + 16].T.reshape(-1) for r in range(8)]).astype(np.int64)
    return lists[np.arange(k) % 512 // 64]


def pack_weight(w):
    k, n = w.shape
    w = f64(np.asarray(w, np.float32).astype(ml_dtypes.bfloat16)).reshape(k // 32, 32, n)
    amax = np.abs(w).max(1)
    byte = np.clip(np.where(amax > 0, np.frexp(amax)[1] - 1 + 127 - 7, 1), 1, 254)
    scaled = (w * np.exp2(127.0 - byte)[:, None, :]).reshape(k, n).astype(np.float32)
    words = np.ascontiguousarray(scaled.reshape(k // 512, 128, 4, n).transpose(0, 1, 3, 2)).astype(ml_dtypes.float8_e4m3fn).view(np.uint8)
    return words, np.ascontiguousarray(byte.astype(np.uint8).reshape(k // 512, 16, n))


def unpack_weight(words, scales):
    g, p, n, _ = words.shape
    vals = np.ascontiguousarray(words).view(ml_dtypes.float8_e4m3fn).astype(np.float64) * np.repeat(np.exp2(scales.astype(np.float64) - 127.0), 8, axis=1)[..., None]
    return vals.transpose(0, 1, 3, 2).reshape(g * 512, n)


def relu(v):
    return np.maximum(v, 0.0)


K, T, S, N, H = 512, 2048, 512, 512, 512


def setup_inputs():
    n = np.random.standard_normal
    s = mx_kscale(K)[:, None]
    u = mx_kscale(H)
    packed_xT = pack_weight(n((K, T)) * s)
    return {
        "x_words": packed_xT[0],
        "x_scales": packed_xT[1],
        "w1": (n((K, H)) / np.sqrt(K) / s).astype(np.float32),
        "gn": (np.random.uniform(0.5, 1.5, (H, 1)) * u[:, None]).astype(np.float32),
        "w2": (n((H, N)) / np.sqrt(H) / u[:, None]).astype(np.float32),
        "offs": striped(np.random.permutation(T)[:S]),
        "x1": striped8(np.stack([np.random.permutation(S) for _ in range(8)])),
        "x2": striped8(np.stack([np.random.permutation(S) for _ in range(8)])),
        "u1": striped8(np.stack([np.random.permutation(S) for _ in range(8)])),
        "u2": striped8(np.stack([np.random.permutation(S) for _ in range(8)])),
    }


def reference(x_words, x_scales, w1, gn, w2, offs, x1, x2, u1, u2):
    xq = unpack_weight(x_words, x_scales)[:, unstriped(offs)]
    y = mxq(f64(w1), 0, "e4m3").T @ xq
    a = relu(y - (np.minimum(y[np.arange(H)[:, None], runs(x1, H)], y[np.arange(H)[:, None], runs(x2, H)])))
    b = relu(y - (np.minimum(y[np.arange(H)[:, None], runs(u1, H)], y[np.arange(H)[:, None], runs(u2, H)])))
    z = f64(gn) * (np.sqrt((a) ** 2 + (b) ** 2 + 0.05))
    return mxq(f64(w2), 0, "e4m3").T @ mxq(z, 0, "e4m3")

@@ -1,0 +1,168 @@
+from contextlib import ExitStack
+
+import concourse.mybir as mybir
+from concourse.masks import make_identity
+
+K, T, S, N, H = 512, 2048, 512, 512, 512
+FLOPS = 2 * K * H * S + 2 * H * N * S
+
+F32 = mybir.dt.float32
+BF16 = mybir.dt.bfloat16
+I32 = mybir.dt.int32
+U32 = mybir.dt.uint32
+U16 = mybir.dt.uint16
+U8 = mybir.dt.uint8
+FP8X4 = mybir.dt.float8_e4m3fn_x4
+ALU = mybir.AluOpType
+ACT = mybir.ActivationFunctionType
+
+P = 128
+PACK = 4
+CHUNKS = [256,128,128]
+
+
+def tile_picked_eikonal_none_p_kernel(tc, x_words, x_scales, w1, gn, w2, offs, x1, x2, u1, u2, out):
+    nc = tc.nc
+    with ExitStack() as ctx:
+        keep = ctx.enter_context(tc.tile_pool(name="keep", bufs=1))
+        work = ctx.enter_context(tc.tile_pool(name="work", bufs=1))
+        psum = ctx.enter_context(tc.psum_pool(name="psum", bufs=1))
+
+        lists = {}
+        for name in ("offs", "x1", "x2", "u1", "u2"):
+            lists[name] = keep.tile([P, S // 16], U16, name="list_" + name)
+
+        xs_all = keep.tile([P, T], U8, align_bytes=64)
+        nc.vector.memset(xs_all[:].bitcast(I32), 0)
+        nc.sync.dma_start(lists["offs"][:], offs)
+        for q in range(4):
+            nc.scalar.dma_start(xs_all[32 * q : 32 * q + 4, :].bitcast(I32), x_scales[0, 4 * q : 4 * q + 4, :].bitcast(I32))
+        warm = keep.tile([P, 2], F32)
+        nc.gpsimd.memset(warm[:, 0:1], 1.0)
+        nc.scalar.activation(warm[:, 1:2], warm[:, 0:1], ACT.Sqrt)
+        xw_all = keep.tile([P, T], I32, align_bytes=64)
+        nc.sync.dma_start(xw_all[:], x_words[0].rearrange("p n t -> p (n t)").bitcast(I32))
+        half = H // 2
+        w1_raw = []
+        for h in range(2):
+            raw = keep.tile([P, PACK, half], F32, name="w1_raw%d" % h)
+            nc.sync.dma_start(raw[:], w1.rearrange("(p j) c -> p j c", j=PACK)[:, :, h * half : (h + 1) * half])
+            w1_raw.append(raw)
+        for name, src in (("x1", x1), ("x2", x2), ("u1", u1), ("u2", u2)):
+            nc.sync.dma_start(lists[name][:], src)
+        w2_raw = keep.tile([P, PACK, N], F32)
+        nc.sync.dma_start(w2_raw[:], w2.rearrange("(p j) c -> p j c", j=PACK))
+        gain = keep.tile([P, PACK], F32)
+        nc.sync.dma_start(gain[:], gn.rearrange("(p t) o -> p (t o)", t=PACK))
+        ident = keep.tile([P, P], F32)
+        make_identity(nc, ident[:])
+
+        xw = keep.tile([P, S], U32, align_bytes=64)
+        xs = keep.tile([P, S], U8, align_bytes=64)
+        nc.vector.tensor_copy(xs[:], xs_all[:].indirect(lists["offs"][:]))
+        nc.vector.tensor_copy(xw[:], xw_all[:].bitcast(U32).indirect(lists["offs"][:]))
+
+        w1_bf = keep.tile([P, PACK, P, PACK], BF16, align_bytes=64)
+        q4 = P // 4
+        nc.scalar.copy(w1_bf[:, :, 0 : 2 * q4, :].rearrange("p t m j -> p m j t"), w1_raw[0][:].rearrange("p j (m t) -> p m j t", t=PACK))
+        nc.scalar.copy(w1_bf[:, :, 2 * q4 : 3 * q4, :].rearrange("p t m j -> p m j t"), w1_raw[1][:, :, 0 : half // 2].rearrange("p j (m t) -> p m j t", t=PACK))
+        nc.vector.tensor_copy(w1_bf[:, :, 3 * q4 :, :].rearrange("p t m j -> p m j t"), w1_raw[1][:, :, half // 2 :].rearrange("p j (m t) -> p m j t", t=PACK))
+        y = []
+        for t in range(PACK):
+            codes = keep.tile([P, P], U32, align_bytes=64, name="w1_codes%d" % t)
+            scales = keep.tile([P, P], U8, align_bytes=64, name="w1_scales%d" % t)
+            nc.vector.quantize_mx(out=codes[:].bitcast(FP8X4), scales=scales[:], in_=w1_bf[:, t, :, :].rearrange("p m j -> p (m j)"))
+            acc = psum.tile([P, S], F32, tag="diff", bufs=3, name="y_acc")
+            nc.tensor.matmul_mx(out=acc[:], lhsT=codes[:].bitcast(FP8X4), lhsT_scale=scales[:], rhs=xw[:].bitcast(FP8X4), rhs_scale=xs[:], start=True, stop=True)
+            yt = keep.tile([P, S], F32, name="y%d" % t)
+            nc.scalar.copy(yt[:], acc[:])
+            y.append(yt)
+
+        w2_bf = keep.tile([P, N, PACK], BF16, align_bytes=64)
+        nc.scalar.copy(w2_bf[:].rearrange("p (c i) t -> p c t i", i=4), w2_raw[:].rearrange("p t (c i) -> p c t i", i=4))
+        w2_codes = keep.tile([P, N], U32, align_bytes=64)
+        w2_scales = keep.tile([P, N], U8, align_bytes=64)
+        out_v = out.rearrange("(g p) n -> p g n", p=P)
+
+        def gathers(c0, w, t):
+            neg = []
+            for k, pair in enumerate((("x1", "u1"), ("x2", "u2"))):
+                tile = work.tile([P, 2, w], F32, tag="neg%d" % k, bufs=2, name="neg%d" % k)
+                neg.append(tile)
+            for ab, pair in enumerate((("x1", "x2"), ("u1", "u2"))):
+                for k in range(2):
+                    nc.vector.tensor_scalar(neg[k][:, ab, :], y[t][:].indirect(lists[pair[k]][:, c0 // 16 : (c0 + w) // 16]), -1.0, 0.0, ALU.mult, ALU.add)
+            return neg
+
+        def slopes(c0, w, t, neg, sums):
+            nsub = w // P
+            top = work.tile([P, 2, w], F32, tag="top", bufs=2)
+            nc.vector.tensor_tensor(top[:], neg[0][:], neg[1][:], ALU.max)
+            diff = psum.tile([P, nsub, 2, P], F32, tag="diff", bufs=3)
+            for s in range(nsub):
+                for ab in range(2):
+                    nc.tensor.matmul(diff[:, s, ab, :], y[t][:, c0 + s * P : c0 + (s + 1) * P], ident[:], start=True, stop=False, is_transpose=True)
+                    nc.tensor.matmul(diff[:, s, ab, :], top[:, ab, s * P : (s + 1) * P], ident[:], start=False, stop=True, is_transpose=True)
+            pos = work.tile([P, nsub, 2, P], F32, tag="pos", bufs=2)
+            nc.scalar.activation(pos[:], diff[:], ACT.Relu)
+            sq = work.tile([P, nsub, 2, P], F32, tag="sq", bufs=2)
+            nc.scalar.activation(sq[:], pos[:], ACT.Square)
+            for s in range(nsub):
+                for ab in range(2):
+                    nc.tensor.matmul(sums[s][:, t, :], sq[:, s, ab, :], ident[:], start=(ab == 0), stop=(ab == 1), is_transpose=True)
+
+        def roots(w, sums):
+            root = work.tile([P, w, PACK], F32, tag="root", bufs=2)
+            for s in range(w // P):
+                nc.scalar.activation(root[:, s * P : (s + 1) * P, :], sums[s][:].rearrange("p t j -> p j t"), ACT.Sqrt, bias=0.05)
+            return root
+
+        def scale(w, root):
+            z = work.tile([P, w, PACK], BF16, tag="z", bufs=2, align_bytes=64)
+            nc.vector.tensor_tensor(z[:], root[:], gain[:].unsqueeze(1).to_broadcast([P, w, PACK]), ALU.mult)
+            return z
+
+        def finish(c0, w, z):
+            codes = work.tile([P, w], U32, tag="z_codes", bufs=2, align_bytes=64)
+            scales = work.tile([P, w], U8, tag="z_scales", bufs=2, align_bytes=64)
+            nc.vector.quantize_mx(out=codes[:].bitcast(FP8X4), scales=scales[:], in_=z[:].rearrange("p j t -> p (j t)"))
+            for h in range(2):
+                acc = psum.tile([P, 2, w], F32, tag="res", bufs=2, name="res_acc")
+                for g in range(2):
+                    m0 = (2 * h + g) * P
+                    nc.tensor.matmul_mx(out=acc[:, g, :], lhsT=w2_codes[:, m0 : m0 + P].bitcast(FP8X4), lhsT_scale=w2_scales[:, m0 : m0 + P], rhs=codes[:].bitcast(FP8X4), rhs_scale=scales[:], start=True, stop=True)
+                res = work.tile([P, 2, w], F32, tag="res_sb", bufs=4)
+                if c0 + w == S and h == 1:
+                    nc.vector.tensor_copy(res[:], acc[:])
+                else:
+                    nc.scalar.copy(res[:], acc[:])
+                nc.sync.dma_start(out_v[:, 2 * h : 2 * h + 2, c0 : c0 + w], res[:])
+
+        units = []
+        c0 = 0
+        for w in CHUNKS:
+            for t in range(PACK):
+                units.append((c0, w, t))
+            c0 = c0 + w
+        pending = None
+        later = []
+        sums_of = {}
+        for i, (c0, w, t) in enumerate(units):
+            if t == 0:
+                sums_of[c0] = [psum.tile([P, PACK, P], F32, tag="sums", bufs=3, name="sums") for s in range(w // P)]
+            neg = gathers(c0, w, t)
+            if pending is not None:
+                slopes(*pending)
+                if pending[2] == PACK - 1:
+                    later.append([0, pending[0], pending[1], roots(pending[1], sums_of[pending[0]])])
+            pending = (c0, w, t, neg, sums_of[c0])
+            if i == 2:
+                nc.vector.quantize_mx(out=w2_codes[:].bitcast(FP8X4), scales=w2_scales[:], in_=w2_bf[:].rearrange("p c t -> p (c t)"))
+            for item in later:
+                item[0] = item[0] + 1
+                if item[0] == 2:
+                    item[3] = scale(item[2], item[3])
+                if item[0] == 3:
+                    finish(item[1], item[2], item[3])
+        slopes(*pending)
+        finish(pending[0], pending[1], scale(pending[1], roots(pending[1], sums_of[pending[0]])))

@@ -18,7 +18,12 @@ ACT = mybir.ActivationFunctionType
 
 P = 128
 PACK = 4
-CHUNKS = [256,128,128]
+WINDOW = 512
+UNITS = [(0, 256, 0, False), (0, 256, 1, False), (0, 256, 2, False), (0, 256, 3, False), (256, 256, 0, False), (256, 256, 1, False), (256, 256, 2, False), (256, 128, 3, False), (384, 128, 3, True)]
+GROUPS = [(0, 256), (256, 128), (384, 128)]
+BUFS = 2
+VM = 80
+TAIL = 256
 
 
 def tile_picked_eikonal_none_p_kernel(tc, x_words, x_scales, w1, gn, w2, offs, x1, x2, u1, u2, out):
@@ -40,15 +45,11 @@ def tile_picked_eikonal_none_p_kernel(tc, x_words, x_scales, w1, gn, w2, offs, x
         warm = keep.tile([P, 2], F32)
         nc.gpsimd.memset(warm[:, 0:1], 1.0)
         nc.scalar.activation(warm[:, 1:2], warm[:, 0:1], ACT.Sqrt)
+        w1_raw = keep.tile([P, PACK, H], F32)
+        nc.sync.dma_start(w1_raw[:], w1.rearrange("(p j) c -> p j c", j=PACK))
         xw_all = keep.tile([P, T], I32, align_bytes=64)
         nc.sync.dma_start(xw_all[:], x_words[0].rearrange("p n t -> p (n t)").bitcast(I32))
-        half = H // 2
-        w1_raw = []
-        for h in range(2):
-            raw = keep.tile([P, PACK, half], F32, name="w1_raw%d" % h)
-            nc.sync.dma_start(raw[:], w1.rearrange("(p j) c -> p j c", j=PACK)[:, :, h * half : (h + 1) * half])
-            w1_raw.append(raw)
-        for name, src in (("x1", x1), ("x2", x2), ("u1", u1), ("u2", u2)):
+        for name, src in (("x1", x1), ("u1", u1), ("x2", x2), ("u2", u2)):
             nc.sync.dma_start(lists[name][:], src)
         w2_raw = keep.tile([P, PACK, N], F32)
         nc.sync.dma_start(w2_raw[:], w2.rearrange("(p j) c -> p j c", j=PACK))
@@ -60,109 +61,129 @@ def tile_picked_eikonal_none_p_kernel(tc, x_words, x_scales, w1, gn, w2, offs, x
         xw = keep.tile([P, S], U32, align_bytes=64)
         xs = keep.tile([P, S], U8, align_bytes=64)
         nc.vector.tensor_copy(xs[:], xs_all[:].indirect(lists["offs"][:]))
-        nc.vector.tensor_copy(xw[:], xw_all[:].bitcast(U32).indirect(lists["offs"][:]))
 
         w1_bf = keep.tile([P, PACK, P, PACK], BF16, align_bytes=64)
-        q4 = P // 4
-        nc.scalar.copy(w1_bf[:, :, 0 : 2 * q4, :].rearrange("p t m j -> p m j t"), w1_raw[0][:].rearrange("p j (m t) -> p m j t", t=PACK))
-        nc.scalar.copy(w1_bf[:, :, 2 * q4 : 3 * q4, :].rearrange("p t m j -> p m j t"), w1_raw[1][:, :, 0 : half // 2].rearrange("p j (m t) -> p m j t", t=PACK))
-        nc.vector.tensor_copy(w1_bf[:, :, 3 * q4 :, :].rearrange("p t m j -> p m j t"), w1_raw[1][:, :, half // 2 :].rearrange("p j (m t) -> p m j t", t=PACK))
+        nc.vector.tensor_copy(w1_bf[:, :, 0:VM, :].rearrange("p t m j -> p m j t"), w1_raw[:, :, 0 : PACK * VM].rearrange("p j (m t) -> p m j t", t=PACK))
+        nc.scalar.copy(w1_bf[:, :, VM:, :].rearrange("p t m j -> p m j t"), w1_raw[:, :, PACK * VM :].rearrange("p j (m t) -> p m j t", t=PACK))
+        w1_codes = keep.tile([P, H], U32, align_bytes=64)
+        w1_scales = keep.tile([P, H], U8, align_bytes=64)
+        nc.vector.quantize_mx(out=w1_codes[:].bitcast(FP8X4), scales=w1_scales[:], in_=w1_bf[:].rearrange("p t m j -> p (t m j)"))
+
+        half = S // 2
+        for h in range(2):
+            nc.vector.tensor_copy(xw[:, h * half : (h + 1) * half], xw_all[:].bitcast(U32).indirect(lists["offs"][:, h * half // 16 : (h + 1) * half // 16]))
         y = []
         for t in range(PACK):
-            codes = keep.tile([P, P], U32, align_bytes=64, name="w1_codes%d" % t)
-            scales = keep.tile([P, P], U8, align_bytes=64, name="w1_scales%d" % t)
-            nc.vector.quantize_mx(out=codes[:].bitcast(FP8X4), scales=scales[:], in_=w1_bf[:, t, :, :].rearrange("p m j -> p (m j)"))
-            acc = psum.tile([P, S], F32, tag="diff", bufs=3, name="y_acc")
-            nc.tensor.matmul_mx(out=acc[:], lhsT=codes[:].bitcast(FP8X4), lhsT_scale=scales[:], rhs=xw[:].bitcast(FP8X4), rhs_scale=xs[:], start=True, stop=True)
-            yt = keep.tile([P, S], F32, name="y%d" % t)
-            nc.scalar.copy(yt[:], acc[:])
+            yt = keep.tile([P, WINDOW], F32, name="y%d" % t)
+
             y.append(yt)
+        for t, c0, w, tag in ((0, 0, half, "diff"), (0, half, half, "diff"), (1, 0, S, "diff"), (2, 0, S, "res"), (3, 0, S, "res")):
+            acc = psum.tile([P, w], F32, tag=tag, bufs=2 if tag == "res" else 3, name="y_acc")
+            nc.tensor.matmul_mx(out=acc[:], lhsT=w1_codes[:, t * P : (t + 1) * P].bitcast(FP8X4), lhsT_scale=w1_scales[:, t * P : (t + 1) * P], rhs=xw[:, c0 : c0 + w].bitcast(FP8X4), rhs_scale=xs[:, c0 : c0 + w], start=True, stop=True)
+            nc.scalar.copy(y[t][:, c0 : c0 + w], acc[:])
 
         w2_bf = keep.tile([P, N, PACK], BF16, align_bytes=64)
         nc.scalar.copy(w2_bf[:].rearrange("p (c i) t -> p c t i", i=4), w2_raw[:].rearrange("p t (c i) -> p c t i", i=4))
         w2_codes = keep.tile([P, N], U32, align_bytes=64)
         w2_scales = keep.tile([P, N], U8, align_bytes=64)
         out_v = out.rearrange("(g p) n -> p g n", p=P)
+        sums = {}
 
         def gathers(c0, w, t):
-            neg = []
-            for k, pair in enumerate((("x1", "u1"), ("x2", "u2"))):
-                tile = work.tile([P, 2, w], F32, tag="neg%d" % k, bufs=2, name="neg%d" % k)
-                neg.append(tile)
-            for ab, pair in enumerate((("x1", "x2"), ("u1", "u2"))):
-                for k in range(2):
-                    nc.vector.tensor_scalar(neg[k][:, ab, :], y[t][:].indirect(lists[pair[k]][:, c0 // 16 : (c0 + w) // 16]), -1.0, 0.0, ALU.mult, ALU.add)
-            return neg
+            cols = slice(c0 // 16, (c0 + w) // 16)
+            neg = work.tile([P, 2, w], F32, tag="neg", bufs=BUFS + 1)
+            gap = work.tile([P, 2, w], F32, tag="gap", bufs=BUFS)
+            for ab, name in enumerate(("x1", "u1")):
+                nc.vector.tensor_scalar(neg[:, ab, :], y[t][:].indirect(lists[name][:, cols]), -1.0, 0.0, ALU.mult, ALU.add)
+            for ab, name in enumerate(("x2", "u2")):
+                nc.vector.tensor_tensor(gap[:, ab, :], y[t][:].indirect(lists[name][:, cols]), neg[:, ab, :], ALU.add)
+            return neg, gap
 
-        def slopes(c0, w, t, neg, sums):
+        def differences(c0, w, t, ab0, nab, neg, gap):
             nsub = w // P
-            top = work.tile([P, 2, w], F32, tag="top", bufs=2)
-            nc.vector.tensor_tensor(top[:], neg[0][:], neg[1][:], ALU.max)
-            diff = psum.tile([P, nsub, 2, P], F32, tag="diff", bufs=3)
+            lift = work.tile([P, nab, w], F32, tag="lift", bufs=2)
+            nc.scalar.activation(lift[:], gap[:, ab0 : ab0 + nab, :], ACT.Relu, scale=-1.0)
+            diff = psum.tile([P, nsub, nab, P], F32, tag="diff", bufs=3)
             for s in range(nsub):
-                for ab in range(2):
-                    nc.tensor.matmul(diff[:, s, ab, :], y[t][:, c0 + s * P : c0 + (s + 1) * P], ident[:], start=True, stop=False, is_transpose=True)
-                    nc.tensor.matmul(diff[:, s, ab, :], top[:, ab, s * P : (s + 1) * P], ident[:], start=False, stop=True, is_transpose=True)
-            pos = work.tile([P, nsub, 2, P], F32, tag="pos", bufs=2)
+                for k in range(nab):
+                    nc.tensor.matmul(diff[:, s, k, :], y[t][:, c0 + s * P : c0 + (s + 1) * P], ident[:], start=True, stop=False, is_transpose=True)
+                    nc.tensor.matmul(diff[:, s, k, :], neg[:, ab0 + k, s * P : (s + 1) * P], ident[:], start=False, stop=False, is_transpose=True)
+                    nc.tensor.matmul(diff[:, s, k, :], lift[:, k, s * P : (s + 1) * P], ident[:], start=False, stop=True, is_transpose=True)
+            return diff
+
+        def squares(c0, w, t, ab0, nab, diff):
+            nsub = w // P
+            pos = work.tile([P, nsub, nab, P], F32, tag="pos", bufs=2)
             nc.scalar.activation(pos[:], diff[:], ACT.Relu)
-            sq = work.tile([P, nsub, 2, P], F32, tag="sq", bufs=2)
+            sq = work.tile([P, nsub, nab, P], F32, tag="sq", bufs=2)
             nc.scalar.activation(sq[:], pos[:], ACT.Square)
             for s in range(nsub):
-                for ab in range(2):
-                    nc.tensor.matmul(sums[s][:, t, :], sq[:, s, ab, :], ident[:], start=(ab == 0), stop=(ab == 1), is_transpose=True)
+                block = c0 // P + s
+                if block not in sums:
+                    sums[block] = psum.tile([P, PACK, P], F32, tag="sums", bufs=3, name="sums")
+                for k in range(nab):
+                    nc.tensor.matmul(sums[block][:, t, :], sq[:, s, k, :], ident[:], start=(ab0 + k == 0), stop=(ab0 + k == 1), is_transpose=True)
 
-        def roots(w, sums):
-            root = work.tile([P, w, PACK], F32, tag="root", bufs=2)
+        def roots(c0, w):
+            root = work.tile([P, w, PACK], F32, tag="root", bufs=3)
             for s in range(w // P):
-                nc.scalar.activation(root[:, s * P : (s + 1) * P, :], sums[s][:].rearrange("p t j -> p j t"), ACT.Sqrt, bias=0.05)
+                nc.scalar.activation(root[:, s * P : (s + 1) * P, :], sums[c0 // P + s][:].rearrange("p t j -> p j t"), ACT.Sqrt, bias=0.05)
             return root
 
         def scale(w, root):
-            z = work.tile([P, w, PACK], BF16, tag="z", bufs=2, align_bytes=64)
+            z = work.tile([P, w, PACK], BF16, tag="z", bufs=3, align_bytes=64)
             nc.vector.tensor_tensor(z[:], root[:], gain[:].unsqueeze(1).to_broadcast([P, w, PACK]), ALU.mult)
             return z
 
         def finish(c0, w, z):
-            codes = work.tile([P, w], U32, tag="z_codes", bufs=2, align_bytes=64)
-            scales = work.tile([P, w], U8, tag="z_scales", bufs=2, align_bytes=64)
+            codes = work.tile([P, w], U32, tag="z_codes", bufs=3, align_bytes=64)
+            scales = work.tile([P, w], U8, tag="z_scales", bufs=3, align_bytes=64)
             nc.vector.quantize_mx(out=codes[:].bitcast(FP8X4), scales=scales[:], in_=z[:].rearrange("p j t -> p (j t)"))
             for h in range(2):
                 acc = psum.tile([P, 2, w], F32, tag="res", bufs=2, name="res_acc")
                 for g in range(2):
                     m0 = (2 * h + g) * P
                     nc.tensor.matmul_mx(out=acc[:, g, :], lhsT=w2_codes[:, m0 : m0 + P].bitcast(FP8X4), lhsT_scale=w2_scales[:, m0 : m0 + P], rhs=codes[:].bitcast(FP8X4), rhs_scale=scales[:], start=True, stop=True)
-                res = work.tile([P, 2, w], F32, tag="res_sb", bufs=4)
-                if c0 + w == S and h == 1:
+                res = work.tile([P, 2, w], F32, tag="res_sb", bufs=6)
+                if c0 >= TAIL and h == 1:
                     nc.vector.tensor_copy(res[:], acc[:])
                 else:
                     nc.scalar.copy(res[:], acc[:])
-                nc.sync.dma_start(out_v[:, 2 * h : 2 * h + 2, c0 : c0 + w], res[:])
+                queue = nc.scalar if (c0 + w == S and h == 0) else nc.sync
+                queue.dma_start(out_v[:, 2 * h : 2 * h + 2, c0 : c0 + w], res[:])
 
-        units = []
-        c0 = 0
-        for w in CHUNKS:
-            for t in range(PACK):
-                units.append((c0, w, t))
-            c0 = c0 + w
-        pending = None
-        later = []
-        sums_of = {}
-        for i, (c0, w, t) in enumerate(units):
-            if t == 0:
-                sums_of[c0] = [psum.tile([P, PACK, P], F32, tag="sums", bufs=3, name="sums") for s in range(w // P)]
-            neg = gathers(c0, w, t)
-            if pending is not None:
-                slopes(*pending)
-                if pending[2] == PACK - 1:
-                    later.append([0, pending[0], pending[1], roots(pending[1], sums_of[pending[0]])])
-            pending = (c0, w, t, neg, sums_of[c0])
+        done = set()
+        rooted, zs = [], []
+        waiting = None
+        got = None
+        for i in range(len(UNITS) + 4):
+            ready_z, ready_r = list(zs), list(rooted)
+            zs.clear()
+            rooted.clear()
+            prev = got
+            got = (UNITS[i], gathers(*UNITS[i][0:3])) if i < len(UNITS) else None
+            steps = []
+            if prev is not None:
+                c0, w, t, split = prev[0]
+                steps = [(c0, w, t, 0, 1), (c0, w, t, 1, 1)] if split else [(c0, w, t, 0, 2)]
+            if not steps and waiting is not None:
+                steps = [None]
+            for step in steps:
+                diff = differences(*step, *prev[1]) if step is not None else None
+                if waiting is not None:
+                    squares(*waiting)
+                    c0, w, t, ab0, nab = waiting[0:5]
+                    if ab0 + nab == 2:
+                        for s in range(w // P):
+                            done.add((c0 // P + s, t))
+                        for g0, gw in GROUPS:
+                            if (g0, "r") not in done and all((b, tt) in done for b in range(g0 // P, (g0 + gw) // P) for tt in range(PACK)):
+                                done.add((g0, "r"))
+                                rooted.append((g0, gw, roots(g0, gw)))
+                waiting = (*step, diff) if step is not None else None
             if i == 2:
                 nc.vector.quantize_mx(out=w2_codes[:].bitcast(FP8X4), scales=w2_scales[:], in_=w2_bf[:].rearrange("p c t -> p (c t)"))
-            for item in later:
-                item[0] = item[0] + 1
-                if item[0] == 2:
-                    item[3] = scale(item[2], item[3])
-                if item[0] == 3:
-                    finish(item[1], item[2], item[3])
-        slopes(*pending)
-        finish(pending[0], pending[1], scale(pending[1], roots(pending[1], sums_of[pending[0]])))
+            for g0, gw, root in ready_r:
+                zs.append((g0, gw, scale(gw, root)))
+            for g0, gw, z in ready_z:
+                finish(g0, gw, z)

@@ -18,172 +18,178 @@ ACT = mybir.ActivationFunctionType
 
 P = 128
 PACK = 4
-WINDOW = 512
-UNITS = [(0, 256, 0, False), (0, 256, 1, False), (0, 256, 2, False), (0, 256, 3, False), (256, 256, 0, False), (256, 256, 1, False), (256, 256, 2, False), (256, 128, 3, False), (384, 128, 3, True)]
-GROUPS = [(0, 256), (256, 128), (384, 128)]
-BUFS = 2
-VM = 80
-TAIL = 256
+HALF = S // 2
+BANK = 512
+LAST_TILE = PACK - 1
+FIRST_LISTS = ("x1", "u1")
+SECOND_LISTS = ("x2", "u2")
+
+W1_VECTOR_COLUMNS = 40
+SLOPE_BANKS = 3
+SUM_BANK = 4
+RING = 2
+
+STEPS = [(c0, HALF, t, (side,)) for c0 in (0, HALF) for t in range(PACK) for side in (0, 1) if (c0, t) != (HALF, LAST_TILE)]
+STEPS = STEPS + [(HALF, P, LAST_TILE, (0, 1)), (HALF + P, P, LAST_TILE, (0,)), (HALF + P, P, LAST_TILE, (1,))]
+GROUPS = [(0, HALF, SUM_BANK), (HALF, P, 0), (HALF + P, P, 2)]
 
 
 def tile_picked_eikonal_none_p_kernel(tc, x_words, x_scales, w1, gn, w2, offs, x1, x2, u1, u2, out):
     nc = tc.nc
     with ExitStack() as ctx:
         keep = ctx.enter_context(tc.tile_pool(name="keep", bufs=1))
-        work = ctx.enter_context(tc.tile_pool(name="work", bufs=1))
         psum = ctx.enter_context(tc.psum_pool(name="psum", bufs=1))
 
         lists = {}
         for name in ("offs", "x1", "x2", "u1", "u2"):
             lists[name] = keep.tile([P, S // 16], U16, name="list_" + name)
+        banks = [psum.tile([P, BANK], F32, name="bank%d" % b) for b in range(8)]
 
         xs_all = keep.tile([P, T], U8, align_bytes=64)
-        nc.vector.memset(xs_all[:].bitcast(I32), 0)
-        nc.sync.dma_start(lists["offs"][:], offs)
+        nc.gpsimd.memset(xs_all[:].bitcast(I32), 0)
         for q in range(4):
             nc.scalar.dma_start(xs_all[32 * q : 32 * q + 4, :].bitcast(I32), x_scales[0, 4 * q : 4 * q + 4, :].bitcast(I32))
-        warm = keep.tile([P, 2], F32)
-        nc.gpsimd.memset(warm[:, 0:1], 1.0)
-        nc.scalar.activation(warm[:, 1:2], warm[:, 0:1], ACT.Sqrt)
-        w1_raw = keep.tile([P, PACK, H], F32)
-        nc.sync.dma_start(w1_raw[:], w1.rearrange("(p j) c -> p j c", j=PACK))
         xw_all = keep.tile([P, T], I32, align_bytes=64)
+        nc.sync.dma_start(lists["offs"][:], offs)
+        nc.sync.dma_start(lists["x1"][:], x1)
         nc.sync.dma_start(xw_all[:], x_words[0].rearrange("p n t -> p (n t)").bitcast(I32))
-        for name, src in (("x1", x1), ("u1", u1), ("x2", x2), ("u2", u2)):
-            nc.sync.dma_start(lists[name][:], src)
+        nc.sync.dma_start(lists["u1"][:], u1)
+        nc.sync.dma_start(lists["x2"][:], x2)
+        w1_rows = w1.rearrange("(p j) c -> p j c", j=PACK)
+        w1_raw = [keep.tile([P, PACK, HALF], F32, name="w1_raw%d" % h) for h in range(2)]
+        for h in range(2):
+            nc.sync.dma_start(w1_raw[h][:], w1_rows[:, :, h * HALF : (h + 1) * HALF])
+        nc.sync.dma_start(lists["u2"][:], u2)
         w2_raw = keep.tile([P, PACK, N], F32)
         nc.sync.dma_start(w2_raw[:], w2.rearrange("(p j) c -> p j c", j=PACK))
         gain = keep.tile([P, PACK], F32)
         nc.sync.dma_start(gain[:], gn.rearrange("(p t) o -> p (t o)", t=PACK))
+        warm = keep.tile([P, 2], F32)
+        nc.vector.memset(warm[:, 0:1], 1.0)
+        nc.scalar.activation(warm[:, 1:2], warm[:, 0:1], ACT.Sqrt)
         ident = keep.tile([P, P], F32)
         make_identity(nc, ident[:])
 
         xw = keep.tile([P, S], U32, align_bytes=64)
         xs = keep.tile([P, S], U8, align_bytes=64)
         nc.vector.tensor_copy(xs[:], xs_all[:].indirect(lists["offs"][:]))
+        for h in range(2):
+            nc.vector.tensor_copy(xw[:, h * HALF : (h + 1) * HALF], xw_all[:].bitcast(U32).indirect(lists["offs"][:, h * HALF // 16 : (h + 1) * HALF // 16]))
 
         w1_bf = keep.tile([P, PACK, P, PACK], BF16, align_bytes=64)
-        nc.vector.tensor_copy(w1_bf[:, :, 0:VM, :].rearrange("p t m j -> p m j t"), w1_raw[:, :, 0 : PACK * VM].rearrange("p j (m t) -> p m j t", t=PACK))
-        nc.scalar.copy(w1_bf[:, :, VM:, :].rearrange("p t m j -> p m j t"), w1_raw[:, :, PACK * VM :].rearrange("p j (m t) -> p m j t", t=PACK))
+
+        def w1_views(h, m0, m1):
+            dst = w1_bf[:, :, h * P // 2 + m0 : h * P // 2 + m1, :].rearrange("p t m j -> p m j t")
+            src = w1_raw[h][:, :, PACK * m0 : PACK * m1].rearrange("p j (m t) -> p m j t", t=PACK)
+            return dst, src
+
+        nc.scalar.copy(*w1_views(0, 0, P // 2))
+        nc.vector.tensor_copy(*w1_views(1, 0, W1_VECTOR_COLUMNS))
+        nc.scalar.copy(*w1_views(1, W1_VECTOR_COLUMNS, P // 2))
         w1_codes = keep.tile([P, H], U32, align_bytes=64)
         w1_scales = keep.tile([P, H], U8, align_bytes=64)
-        nc.vector.quantize_mx(out=w1_codes[:].bitcast(FP8X4), scales=w1_scales[:], in_=w1_bf[:].rearrange("p t m j -> p (t m j)"))
+        for t0, t1 in ((0, 1), (1, 2), (2, PACK)):
+            nc.vector.quantize_mx(out=w1_codes[:, t0 * P : t1 * P].bitcast(FP8X4), scales=w1_scales[:, t0 * P : t1 * P], in_=w1_bf[:, t0:t1, :, :].rearrange("p t m j -> p (t m j)"))
 
-        half = S // 2
-        for h in range(2):
-            nc.vector.tensor_copy(xw[:, h * half : (h + 1) * half], xw_all[:].bitcast(U32).indirect(lists["offs"][:, h * half // 16 : (h + 1) * half // 16]))
-        y = []
-        for t in range(PACK):
-            yt = keep.tile([P, WINDOW], F32, name="y%d" % t)
+        y = [keep.tile([P, S], F32, name="y%d" % t) for t in range(PACK)]
+        pieces = [(0, 0, HALF), (0, HALF, HALF)] + [(t, 0, S) for t in range(1, PACK)]
+        for b, (t, c0, w) in enumerate(pieces):
+            acc = banks[SLOPE_BANKS + b][:, 0:w]
+            nc.tensor.matmul_mx(out=acc, lhsT=w1_codes[:, t * P : (t + 1) * P].bitcast(FP8X4), lhsT_scale=w1_scales[:, t * P : (t + 1) * P], rhs=xw[:, c0 : c0 + w].bitcast(FP8X4), rhs_scale=xs[:, c0 : c0 + w], start=True, stop=True)
+            if c0 == HALF:
+                nc.vector.tensor_copy(y[t][:, c0 : c0 + w], acc)
+            else:
+                nc.scalar.copy(y[t][:, c0 : c0 + w], acc)
 
-            y.append(yt)
-        for t, c0, w, tag in ((0, 0, half, "diff"), (0, half, half, "diff"), (1, 0, S, "diff"), (2, 0, S, "res"), (3, 0, S, "res")):
-            acc = psum.tile([P, w], F32, tag=tag, bufs=2 if tag == "res" else 3, name="y_acc")
-            nc.tensor.matmul_mx(out=acc[:], lhsT=w1_codes[:, t * P : (t + 1) * P].bitcast(FP8X4), lhsT_scale=w1_scales[:, t * P : (t + 1) * P], rhs=xw[:, c0 : c0 + w].bitcast(FP8X4), rhs_scale=xs[:, c0 : c0 + w], start=True, stop=True)
-            nc.scalar.copy(y[t][:, c0 : c0 + w], acc[:])
+        neg = [keep.tile([P, 2, S], F32, align_bytes=64, tag="neg%d" % t, name="neg%d" % t) for t in range(PACK)]
+        gap = [keep.tile([P, 2, S], F32, align_bytes=64, tag="gap%d" % t, name="gap%d" % t) for t in range(PACK)]
+        lift = [keep.tile([P, HALF], F32, name="lift%d" % i) for i in range(RING)]
+        pos = [keep.tile([P, HALF], F32, align_bytes=64, tag="pos%d" % i, name="pos%d" % i) for i in range(RING)]
+        square = [keep.tile([P, HALF], F32, name="square%d" % i) for i in range(RING)]
+        root = keep.tile([P, S, PACK], F32)
+        last = len(STEPS) - 1
 
-        w2_bf = keep.tile([P, N, PACK], BF16, align_bytes=64)
-        nc.scalar.copy(w2_bf[:].rearrange("p (c i) t -> p c t i", i=4), w2_raw[:].rearrange("p t (c i) -> p c t i", i=4))
-        w2_codes = keep.tile([P, N], U32, align_bytes=64)
-        w2_scales = keep.tile([P, N], U8, align_bytes=64)
-        out_v = out.rearrange("(g p) n -> p g n", p=P)
-        sums = {}
+        def gather_first(c0, w, t):
+            for side, name in enumerate(FIRST_LISTS):
+                nc.vector.tensor_scalar(neg[t][:, side, c0 : c0 + w], y[t][:].indirect(lists[name][:, c0 // 16 : (c0 + w) // 16]), -1.0, 0.0, ALU.mult, ALU.add)
 
-        def gathers(c0, w, t):
-            cols = slice(c0 // 16, (c0 + w) // 16)
-            neg = work.tile([P, 2, w], F32, tag="neg", bufs=BUFS + 1)
-            gap = work.tile([P, 2, w], F32, tag="gap", bufs=BUFS)
-            for ab, name in enumerate(("x1", "u1")):
-                nc.vector.tensor_scalar(neg[:, ab, :], y[t][:].indirect(lists[name][:, cols]), -1.0, 0.0, ALU.mult, ALU.add)
-            for ab, name in enumerate(("x2", "u2")):
-                nc.vector.tensor_tensor(gap[:, ab, :], y[t][:].indirect(lists[name][:, cols]), neg[:, ab, :], ALU.add)
-            return neg, gap
+        def gather_second(c0, w, t):
+            for side, name in enumerate(SECOND_LISTS):
+                nc.vector.tensor_tensor(gap[t][:, side, c0 : c0 + w], y[t][:].indirect(lists[name][:, c0 // 16 : (c0 + w) // 16]), neg[t][:, side, c0 : c0 + w], ALU.add)
 
-        def differences(c0, w, t, ab0, nab, neg, gap):
-            nsub = w // P
-            lift = work.tile([P, nab, w], F32, tag="lift", bufs=2)
-            nc.scalar.activation(lift[:], gap[:, ab0 : ab0 + nab, :], ACT.Relu, scale=-1.0)
-            diff = psum.tile([P, nsub, nab, P], F32, tag="diff", bufs=3)
-            for s in range(nsub):
-                for k in range(nab):
-                    nc.tensor.matmul(diff[:, s, k, :], y[t][:, c0 + s * P : c0 + (s + 1) * P], ident[:], start=True, stop=False, is_transpose=True)
-                    nc.tensor.matmul(diff[:, s, k, :], neg[:, ab0 + k, s * P : (s + 1) * P], ident[:], start=False, stop=False, is_transpose=True)
-                    nc.tensor.matmul(diff[:, s, k, :], lift[:, k, s * P : (s + 1) * P], ident[:], start=False, stop=True, is_transpose=True)
-            return diff
+        def gathers(c0, t):
+            cuts = [(c0, P), (c0 + P, P)] if (c0, t) == (HALF, LAST_TILE) else [(c0, HALF)]
+            for cut in cuts:
+                gather_first(*cut, t)
+            for cut in cuts:
+                gather_second(*cut, t)
 
-        def squares(c0, w, t, ab0, nab, diff):
-            nsub = w // P
-            pos = work.tile([P, nsub, nab, P], F32, tag="pos", bufs=2)
-            nc.scalar.activation(pos[:], diff[:], ACT.Relu)
-            sq = work.tile([P, nsub, nab, P], F32, tag="sq", bufs=2)
-            nc.scalar.activation(sq[:], pos[:], ACT.Square)
-            for s in range(nsub):
-                block = c0 // P + s
-                if block not in sums:
-                    sums[block] = psum.tile([P, PACK, P], F32, tag="sums", bufs=3, name="sums")
-                for k in range(nab):
-                    nc.tensor.matmul(sums[block][:, t, :], sq[:, s, k, :], ident[:], start=(ab0 + k == 0), stop=(ab0 + k == 1), is_transpose=True)
+        def squares_of(i):
+            c0, w, t, sides = STEPS[i]
+            found = [(c, side) for side in sides for c in range(c0, c0 + w, P)]
+            return [(slice(n * P, (n + 1) * P), c, side) for n, (c, side) in enumerate(found)]
+
+        def add_own_and_first(i):
+            t = STEPS[i][2]
+            for place, c, side in squares_of(i):
+                nc.tensor.matmul(banks[i % SLOPE_BANKS][:, place], y[t][:, c : c + P], ident[:], start=(place.start == 0), stop=False, is_transpose=True)
+                nc.tensor.matmul(banks[i % SLOPE_BANKS][:, place], neg[t][:, side, c : c + P], ident[:], start=False, stop=False, is_transpose=True)
+
+        def add_lift(i):
+            c0, w, t, sides = STEPS[i]
+            width = w * len(sides)
+            nc.scalar.activation(lift[i % RING][:, 0:width].rearrange("p (k j) -> p k j", k=len(sides)), gap[t][:, sides[0] : sides[-1] + 1, c0 : c0 + w], ACT.Relu, scale=-1.0)
+            for place, c, side in squares_of(i):
+                nc.tensor.matmul(banks[i % SLOPE_BANKS][:, place], lift[i % RING][:, place], ident[:], start=False, stop=(place.stop == width), is_transpose=True)
+
+        def square_and_turn_back(i):
+            c0, w, t, sides = STEPS[i]
+            width = w * len(sides)
+            nc.scalar.activation(pos[i % RING][:, 0:width], banks[i % SLOPE_BANKS][:, 0:width], ACT.Relu)
+            nc.scalar.activation(square[i % RING][:, 0:width], pos[i % RING][:, 0:width], ACT.Square)
+            for place, c, side in squares_of(i):
+                nc.tensor.matmul(banks[SUM_BANK + c // P][:, t * P : (t + 1) * P], square[i % RING][:, place], ident[:], start=(side == 0), stop=(side == 1), is_transpose=True)
 
         def roots(c0, w):
-            root = work.tile([P, w, PACK], F32, tag="root", bufs=3)
-            for s in range(w // P):
-                nc.scalar.activation(root[:, s * P : (s + 1) * P, :], sums[c0 // P + s][:].rearrange("p t j -> p j t"), ACT.Sqrt, bias=0.05)
-            return root
+            for b in range(c0 // P, (c0 + w) // P):
+                nc.scalar.activation(root[:, b * P : (b + 1) * P, :], banks[SUM_BANK + b][:].rearrange("p (t j) -> p j t", t=PACK), ACT.Sqrt, bias=0.05)
 
-        def scale(w, root):
-            z = work.tile([P, w, PACK], BF16, tag="z", bufs=3, align_bytes=64)
-            nc.vector.tensor_tensor(z[:], root[:], gain[:].unsqueeze(1).to_broadcast([P, w, PACK]), ALU.mult)
-            return z
+        for i in range(last + 2):
+            if i <= last:
+                c0, w, t, sides = STEPS[i]
+                if c0 % HALF == 0 and sides[0] == 0:
+                    gathers(c0, t)
+                add_own_and_first(i)
+                add_lift(i)
+            if i >= 1:
+                square_and_turn_back(i - 1)
+                c0, w, t, sides = STEPS[i - 1]
+                if t == LAST_TILE and sides[-1] == 1:
+                    roots(c0, w)
 
-        def finish(c0, w, z):
-            codes = work.tile([P, w], U32, tag="z_codes", bufs=3, align_bytes=64)
-            scales = work.tile([P, w], U8, tag="z_scales", bufs=3, align_bytes=64)
-            nc.vector.quantize_mx(out=codes[:].bitcast(FP8X4), scales=scales[:], in_=z[:].rearrange("p j t -> p (j t)"))
+        w2_codes = keep.tile([P, N], U32, align_bytes=64, tag="gap2", name="w2_codes")
+        w2_scales = keep.tile([P, N], U8, align_bytes=64)
+        w2_bf = keep.tile([P, N, PACK], BF16, align_bytes=64, tag="neg2", name="w2_bf")
+        nc.vector.tensor_copy(w2_bf[:].rearrange("p (c i) t -> p c t i", i=4), w2_raw[:].rearrange("p t (c i) -> p c t i", i=4))
+        nc.vector.quantize_mx(out=w2_codes[:].bitcast(FP8X4), scales=w2_scales[:], in_=w2_bf[:].rearrange("p c t -> p (c t)"))
+        z = keep.tile([P, S, PACK], BF16, align_bytes=64, tag="neg1", name="z")
+        z_codes = keep.tile([P, S], U32, align_bytes=64, tag="pos%d" % (last % RING), name="z_codes")
+        z_scales = keep.tile([P, S], U8, align_bytes=64)
+        for c0, w, bank0 in GROUPS:
+            nc.vector.tensor_tensor(z[:, c0 : c0 + w, :], root[:, c0 : c0 + w, :], gain[:].unsqueeze(1).to_broadcast([P, w, PACK]), ALU.mult)
+        out_v = out.rearrange("(g p) n -> p g n", p=P)
+        for c0, w, bank0 in GROUPS:
+            cols = slice(c0, c0 + w)
+            nc.vector.quantize_mx(out=z_codes[:, cols].bitcast(FP8X4), scales=z_scales[:, cols], in_=z[:, cols, :].rearrange("p j t -> p (j t)"))
             for h in range(2):
-                acc = psum.tile([P, 2, w], F32, tag="res", bufs=2, name="res_acc")
+                acc = banks[bank0 + h]
                 for g in range(2):
-                    m0 = (2 * h + g) * P
-                    nc.tensor.matmul_mx(out=acc[:, g, :], lhsT=w2_codes[:, m0 : m0 + P].bitcast(FP8X4), lhsT_scale=w2_scales[:, m0 : m0 + P], rhs=codes[:].bitcast(FP8X4), rhs_scale=scales[:], start=True, stop=True)
-                res = work.tile([P, 2, w], F32, tag="res_sb", bufs=6)
-                if c0 >= TAIL and h == 1:
-                    nc.vector.tensor_copy(res[:], acc[:])
+                    rows = slice((2 * h + g) * P, (2 * h + g + 1) * P)
+                    nc.tensor.matmul_mx(out=acc[:, g * w : (g + 1) * w], lhsT=w2_codes[:, rows].bitcast(FP8X4), lhsT_scale=w2_scales[:, rows], rhs=z_codes[:, cols].bitcast(FP8X4), rhs_scale=z_scales[:, cols], start=True, stop=True)
+                res = keep.tile([P, 2, w], F32, name="res%d_%d" % (c0, h))
+                if c0 > 0 and h == 1:
+                    nc.vector.tensor_copy(res[:], acc[:, 0 : 2 * w].rearrange("p (g j) -> p g j", g=2))
                 else:
-                    nc.scalar.copy(res[:], acc[:])
+                    nc.scalar.copy(res[:], acc[:, 0 : 2 * w].rearrange("p (g j) -> p g j", g=2))
                 queue = nc.scalar if (c0 + w == S and h == 0) else nc.sync
-                queue.dma_start(out_v[:, 2 * h : 2 * h + 2, c0 : c0 + w], res[:])
-
-        done = set()
-        rooted, zs = [], []
-        waiting = None
-        got = None
-        for i in range(len(UNITS) + 4):
-            ready_z, ready_r = list(zs), list(rooted)
-            zs.clear()
-            rooted.clear()
-            prev = got
-            got = (UNITS[i], gathers(*UNITS[i][0:3])) if i < len(UNITS) else None
-            steps = []
-            if prev is not None:
-                c0, w, t, split = prev[0]
-                steps = [(c0, w, t, 0, 1), (c0, w, t, 1, 1)] if split else [(c0, w, t, 0, 2)]
-            if not steps and waiting is not None:
-                steps = [None]
-            for step in steps:
-                diff = differences(*step, *prev[1]) if step is not None else None
-                if waiting is not None:
-                    squares(*waiting)
-                    c0, w, t, ab0, nab = waiting[0:5]
-                    if ab0 + nab == 2:
-                        for s in range(w // P):
-                            done.add((c0 // P + s, t))
-                        for g0, gw in GROUPS:
-                            if (g0, "r") not in done and all((b, tt) in done for b in range(g0 // P, (g0 + gw) // P) for tt in range(PACK)):
-                                done.add((g0, "r"))
-                                rooted.append((g0, gw, roots(g0, gw)))
-                waiting = (*step, diff) if step is not None else None
-            if i == 2:
-                nc.vector.quantize_mx(out=w2_codes[:].bitcast(FP8X4), scales=w2_scales[:], in_=w2_bf[:].rearrange("p c t -> p (c t)"))
-            for g0, gw, root in ready_r:
-                zs.append((g0, gw, scale(gw, root)))
-            for g0, gw, z in ready_z:
-                finish(g0, gw, z)
+                queue.dma_start(out_v[:, 2 * h : 2 * h + 2, cols], res[:])

@@ -30,7 +30,8 @@ SUM_BANK = 4
 RING = 2
 
 STEPS = [(c0, HALF, t, (side,)) for c0 in (0, HALF) for t in range(PACK) for side in (0, 1) if (c0, t) != (HALF, LAST_TILE)]
-STEPS = STEPS + [(HALF, P, LAST_TILE, (0, 1)), (HALF + P, P, LAST_TILE, (0,)), (HALF + P, P, LAST_TILE, (1,))]
+STEPS = STEPS + [(HALF, P, LAST_TILE, (0, 1))]
+LAST_BLOCK = slice(S - P, S)
 GROUPS = [(0, HALF, SUM_BANK), (HALF, P, 0), (HALF + P, P, 2)]
 
 
@@ -100,29 +101,24 @@ def tile_picked_eikonal_none_p_kernel(tc, x_words, x_scales, w1, gn, w2, offs, x
                 nc.vector.tensor_copy(y[t][:, c0 : c0 + w], acc)
             else:
                 nc.scalar.copy(y[t][:, c0 : c0 + w], acc)
+        own = keep.tile([P, P], F32)
+        nc.scalar.copy(own[:], banks[SLOPE_BANKS + PACK][:, LAST_BLOCK])
 
         neg = [keep.tile([P, 2, S], F32, align_bytes=64, tag="neg%d" % t, name="neg%d" % t) for t in range(PACK)]
         gap = [keep.tile([P, 2, S], F32, align_bytes=64, tag="gap%d" % t, name="gap%d" % t) for t in range(PACK)]
         lift = [keep.tile([P, HALF], F32, name="lift%d" % i) for i in range(RING)]
         pos = [keep.tile([P, HALF], F32, align_bytes=64, tag="pos%d" % i, name="pos%d" % i) for i in range(RING)]
-        square = [keep.tile([P, HALF], F32, name="square%d" % i) for i in range(RING)]
-        root = keep.tile([P, S, PACK], F32)
+        square = [keep.tile([P, HALF], F32, align_bytes=64, tag="square%d" % i, name="square%d" % i) for i in range(RING)]
+        root = keep.tile([P, S - P, PACK], F32)
+        w2_bf = keep.tile([P, N, PACK], BF16, align_bytes=64)
         last = len(STEPS) - 1
 
-        def gather_first(c0, w, t):
+        def gathers(c0, w, t):
+            entries = slice(c0 // 16, (c0 + w) // 16)
             for side, name in enumerate(FIRST_LISTS):
-                nc.vector.tensor_scalar(neg[t][:, side, c0 : c0 + w], y[t][:].indirect(lists[name][:, c0 // 16 : (c0 + w) // 16]), -1.0, 0.0, ALU.mult, ALU.add)
-
-        def gather_second(c0, w, t):
+                nc.vector.tensor_scalar(neg[t][:, side, c0 : c0 + w], y[t][:].indirect(lists[name][:, entries]), -1.0, 0.0, ALU.mult, ALU.add)
             for side, name in enumerate(SECOND_LISTS):
-                nc.vector.tensor_tensor(gap[t][:, side, c0 : c0 + w], y[t][:].indirect(lists[name][:, c0 // 16 : (c0 + w) // 16]), neg[t][:, side, c0 : c0 + w], ALU.add)
-
-        def gathers(c0, t):
-            cuts = [(c0, P), (c0 + P, P)] if (c0, t) == (HALF, LAST_TILE) else [(c0, HALF)]
-            for cut in cuts:
-                gather_first(*cut, t)
-            for cut in cuts:
-                gather_second(*cut, t)
+                nc.vector.tensor_tensor(gap[t][:, side, c0 : c0 + w], y[t][:].indirect(lists[name][:, entries]), neg[t][:, side, c0 : c0 + w], ALU.add)
 
         def squares_of(i):
             c0, w, t, sides = STEPS[i]
@@ -157,26 +153,43 @@ def tile_picked_eikonal_none_p_kernel(tc, x_words, x_scales, w1, gn, w2, offs, x
         for i in range(last + 2):
             if i <= last:
                 c0, w, t, sides = STEPS[i]
-                if c0 % HALF == 0 and sides[0] == 0:
-                    gathers(c0, t)
+                if sides[0] == 0:
+                    gathers(c0, w, t)
                 add_own_and_first(i)
                 add_lift(i)
+            if i < N // P:
+                cols = slice(i * P, (i + 1) * P)
+                nc.scalar.copy(w2_bf[:, cols, :].rearrange("p (c i) t -> p c t i", i=4), w2_raw[:, :, cols].rearrange("p t (c i) -> p c t i", i=4))
             if i >= 1:
                 square_and_turn_back(i - 1)
                 c0, w, t, sides = STEPS[i - 1]
                 if t == LAST_TILE and sides[-1] == 1:
                     roots(c0, w)
 
+
+        rise = keep.tile([P, 2, 2, P], F32, align_bytes=64, tag="neg0", name="rise")
+        for side in range(2):
+            for k, name in enumerate((FIRST_LISTS[side], SECOND_LISTS[side])):
+                nc.vector.tensor_tensor(rise[:, k, side, :], y[LAST_TILE][:].indirect(lists[name][:, (S - P) // 16 :]), own[:], ALU.subtract)
+        drop = keep.tile([P, 2, P], F32)
+        nc.vector.scalar_tensor_tensor(drop[:], rise[:, 0, :, :], 0.0, rise[:, 1, :, :], ALU.min, ALU.min)
+        drop_square = keep.tile([P, 2, P], F32)
+        nc.vector.tensor_tensor(drop_square[:], drop[:], drop[:], ALU.mult)
+        total = keep.tile([P, P], F32)
+        nc.vector.tensor_tensor(total[:], drop_square[:, 0, :], drop_square[:, 1, :], ALU.add)
+        last_root = keep.tile([P, PACK, P], F32, align_bytes=64, tag="square%d" % (last % RING), name="last_root")
+        nc.scalar.activation(last_root[:, 0:LAST_TILE, :], banks[SUM_BANK + PACK - 1][:, 0 : LAST_TILE * P].rearrange("p (t j) -> p t j", t=LAST_TILE), ACT.Sqrt, bias=0.05)
+        nc.scalar.activation(last_root[:, LAST_TILE, :], total[:], ACT.Sqrt, bias=0.05)
+
         w2_codes = keep.tile([P, N], U32, align_bytes=64, tag="gap2", name="w2_codes")
         w2_scales = keep.tile([P, N], U8, align_bytes=64)
-        w2_bf = keep.tile([P, N, PACK], BF16, align_bytes=64, tag="neg2", name="w2_bf")
-        nc.vector.tensor_copy(w2_bf[:].rearrange("p (c i) t -> p c t i", i=4), w2_raw[:].rearrange("p t (c i) -> p c t i", i=4))
         nc.vector.quantize_mx(out=w2_codes[:].bitcast(FP8X4), scales=w2_scales[:], in_=w2_bf[:].rearrange("p c t -> p (c t)"))
         z = keep.tile([P, S, PACK], BF16, align_bytes=64, tag="neg1", name="z")
         z_codes = keep.tile([P, S], U32, align_bytes=64, tag="pos%d" % (last % RING), name="z_codes")
         z_scales = keep.tile([P, S], U8, align_bytes=64)
         for c0, w, bank0 in GROUPS:
-            nc.vector.tensor_tensor(z[:, c0 : c0 + w, :], root[:, c0 : c0 + w, :], gain[:].unsqueeze(1).to_broadcast([P, w, PACK]), ALU.mult)
+            src = root[:, c0 : c0 + w, :] if c0 + w < S else last_root[:].rearrange("p t j -> p j t")
+            nc.vector.tensor_tensor(z[:, c0 : c0 + w, :], src, gain[:].unsqueeze(1).to_broadcast([P, w, PACK]), ALU.mult)
         out_v = out.rearrange("(g p) n -> p g n", p=P)
         for c0, w, bank0 in GROUPS:
             cols = slice(c0, c0 + w)

from contextlib import ExitStack

import concourse.mybir as mybir
from concourse.masks import make_identity

K, T, S, N, H = 512, 2048, 512, 512, 512
FLOPS = 2 * K * H * S + 2 * H * N * S

F32 = mybir.dt.float32
BF16 = mybir.dt.bfloat16
I32 = mybir.dt.int32
U32 = mybir.dt.uint32
U16 = mybir.dt.uint16
U8 = mybir.dt.uint8
FP8X4 = mybir.dt.float8_e4m3fn_x4
ALU = mybir.AluOpType
ACT = mybir.ActivationFunctionType

P = 128
PACK = 4
HALF = S // 2
BANK = 512
LAST_TILE = PACK - 1
FIRST_LISTS = ("x1", "u1")
SECOND_LISTS = ("x2", "u2")

W1_VECTOR_COLUMNS = 40
SLOPE_BANKS = 3
SUM_BANK = 4
RING = 2

STEPS = [(c0, HALF, t, (side,)) for c0 in (0, HALF) for t in range(PACK) for side in (0, 1) if (c0, t) != (HALF, LAST_TILE)]
STEPS = STEPS + [(HALF, P, LAST_TILE, (0, 1))]
LAST_BLOCK = slice(S - P, S)
GROUPS = [(0, HALF, SUM_BANK), (HALF, P, 0), (HALF + P, P, 2)]


def tile_picked_eikonal_none_p_kernel(tc, x_words, x_scales, w1, gn, w2, offs, x1, x2, u1, u2, out):
    nc = tc.nc
    with ExitStack() as ctx:
        keep = ctx.enter_context(tc.tile_pool(name="keep", bufs=1))
        psum = ctx.enter_context(tc.psum_pool(name="psum", bufs=1))

        lists = {}
        for name in ("offs", "x1", "x2", "u1", "u2"):
            lists[name] = keep.tile([P, S // 16], U16, name="list_" + name)
        banks = [psum.tile([P, BANK], F32, name="bank%d" % b) for b in range(8)]

        xs_all = keep.tile([P, T], U8, align_bytes=64)
        nc.gpsimd.memset(xs_all[:].bitcast(I32), 0)
        for q in range(4):
            nc.scalar.dma_start(xs_all[32 * q : 32 * q + 4, :].bitcast(I32), x_scales[0, 4 * q : 4 * q + 4, :].bitcast(I32))
        xw_all = keep.tile([P, T], I32, align_bytes=64)
        nc.sync.dma_start(lists["offs"][:], offs)
        nc.sync.dma_start(lists["x1"][:], x1)
        nc.sync.dma_start(xw_all[:], x_words[0].rearrange("p n t -> p (n t)").bitcast(I32))
        nc.sync.dma_start(lists["u1"][:], u1)
        nc.sync.dma_start(lists["x2"][:], x2)
        w1_rows = w1.rearrange("(p j) c -> p j c", j=PACK)
        w1_raw = [keep.tile([P, PACK, HALF], F32, name="w1_raw%d" % h) for h in range(2)]
        for h in range(2):
            nc.sync.dma_start(w1_raw[h][:], w1_rows[:, :, h * HALF : (h + 1) * HALF])
        nc.sync.dma_start(lists["u2"][:], u2)
        w2_raw = keep.tile([P, PACK, N], F32)
        nc.sync.dma_start(w2_raw[:], w2.rearrange("(p j) c -> p j c", j=PACK))
        gain = keep.tile([P, PACK], F32)
        nc.sync.dma_start(gain[:], gn.rearrange("(p t) o -> p (t o)", t=PACK))
        warm = keep.tile([P, 2], F32)
        nc.vector.memset(warm[:, 0:1], 1.0)
        nc.scalar.activation(warm[:, 1:2], warm[:, 0:1], ACT.Sqrt)
        ident = keep.tile([P, P], F32)
        make_identity(nc, ident[:])

        xw = keep.tile([P, S], U32, align_bytes=64)
        xs = keep.tile([P, S], U8, align_bytes=64)
        nc.vector.tensor_copy(xs[:], xs_all[:].indirect(lists["offs"][:]))
        for h in range(2):
            nc.vector.tensor_copy(xw[:, h * HALF : (h + 1) * HALF], xw_all[:].bitcast(U32).indirect(lists["offs"][:, h * HALF // 16 : (h + 1) * HALF // 16]))

        w1_bf = keep.tile([P, PACK, P, PACK], BF16, align_bytes=64)

        def w1_views(h, m0, m1):
            dst = w1_bf[:, :, h * P // 2 + m0 : h * P // 2 + m1, :].rearrange("p t m j -> p m j t")
            src = w1_raw[h][:, :, PACK * m0 : PACK * m1].rearrange("p j (m t) -> p m j t", t=PACK)
            return dst, src

        nc.scalar.copy(*w1_views(0, 0, P // 2))
        nc.vector.tensor_copy(*w1_views(1, 0, W1_VECTOR_COLUMNS))
        nc.scalar.copy(*w1_views(1, W1_VECTOR_COLUMNS, P // 2))
        w1_codes = keep.tile([P, H], U32, align_bytes=64)
        w1_scales = keep.tile([P, H], U8, align_bytes=64)
        for t0, t1 in ((0, 1), (1, 2), (2, PACK)):
            nc.vector.quantize_mx(out=w1_codes[:, t0 * P : t1 * P].bitcast(FP8X4), scales=w1_scales[:, t0 * P : t1 * P], in_=w1_bf[:, t0:t1, :, :].rearrange("p t m j -> p (t m j)"))

        y = [keep.tile([P, S], F32, name="y%d" % t) for t in range(PACK)]
        pieces = [(0, 0, HALF), (0, HALF, HALF)] + [(t, 0, S) for t in range(1, PACK)]
        for b, (t, c0, w) in enumerate(pieces):
            acc = banks[SLOPE_BANKS + b][:, 0:w]
            nc.tensor.matmul_mx(out=acc, lhsT=w1_codes[:, t * P : (t + 1) * P].bitcast(FP8X4), lhsT_scale=w1_scales[:, t * P : (t + 1) * P], rhs=xw[:, c0 : c0 + w].bitcast(FP8X4), rhs_scale=xs[:, c0 : c0 + w], start=True, stop=True)
            if c0 == HALF:
                nc.vector.tensor_copy(y[t][:, c0 : c0 + w], acc)
            else:
                nc.scalar.copy(y[t][:, c0 : c0 + w], acc)
        own = keep.tile([P, P], F32)
        nc.scalar.copy(own[:], banks[SLOPE_BANKS + PACK][:, LAST_BLOCK])

        neg = [keep.tile([P, 2, S], F32, align_bytes=64, tag="neg%d" % t, name="neg%d" % t) for t in range(PACK)]
        gap = [keep.tile([P, 2, S], F32, align_bytes=64, tag="gap%d" % t, name="gap%d" % t) for t in range(PACK)]
        lift = [keep.tile([P, HALF], F32, name="lift%d" % i) for i in range(RING)]
        pos = [keep.tile([P, HALF], F32, align_bytes=64, tag="pos%d" % i, name="pos%d" % i) for i in range(RING)]
        square = [keep.tile([P, HALF], F32, align_bytes=64, tag="square%d" % i, name="square%d" % i) for i in range(RING)]
        root = keep.tile([P, S - P, PACK], F32)
        w2_bf = keep.tile([P, N, PACK], BF16, align_bytes=64)
        last = len(STEPS) - 1

        def gathers(c0, w, t):
            entries = slice(c0 // 16, (c0 + w) // 16)
            for side, name in enumerate(FIRST_LISTS):
                nc.vector.tensor_scalar(neg[t][:, side, c0 : c0 + w], y[t][:].indirect(lists[name][:, entries]), -1.0, 0.0, ALU.mult, ALU.add)
            for side, name in enumerate(SECOND_LISTS):
                nc.vector.tensor_tensor(gap[t][:, side, c0 : c0 + w], y[t][:].indirect(lists[name][:, entries]), neg[t][:, side, c0 : c0 + w], ALU.add)

        def squares_of(i):
            c0, w, t, sides = STEPS[i]
            found = [(c, side) for side in sides for c in range(c0, c0 + w, P)]
            return [(slice(n * P, (n + 1) * P), c, side) for n, (c, side) in enumerate(found)]

        def add_own_and_first(i):
            t = STEPS[i][2]
            for place, c, side in squares_of(i):
                nc.tensor.matmul(banks[i % SLOPE_BANKS][:, place], y[t][:, c : c + P], ident[:], start=(place.start == 0), stop=False, is_transpose=True)
                nc.tensor.matmul(banks[i % SLOPE_BANKS][:, place], neg[t][:, side, c : c + P], ident[:], start=False, stop=False, is_transpose=True)

        def add_lift(i):
            c0, w, t, sides = STEPS[i]
            width = w * len(sides)
            nc.scalar.activation(lift[i % RING][:, 0:width].rearrange("p (k j) -> p k j", k=len(sides)), gap[t][:, sides[0] : sides[-1] + 1, c0 : c0 + w], ACT.Relu, scale=-1.0)
            for place, c, side in squares_of(i):
                nc.tensor.matmul(banks[i % SLOPE_BANKS][:, place], lift[i % RING][:, place], ident[:], start=False, stop=(place.stop == width), is_transpose=True)

        def square_and_turn_back(i):
            c0, w, t, sides = STEPS[i]
            width = w * len(sides)
            nc.scalar.activation(pos[i % RING][:, 0:width], banks[i % SLOPE_BANKS][:, 0:width], ACT.Relu)
            nc.scalar.activation(square[i % RING][:, 0:width], pos[i % RING][:, 0:width], ACT.Square)
            for place, c, side in squares_of(i):
                nc.tensor.matmul(banks[SUM_BANK + c // P][:, t * P : (t + 1) * P], square[i % RING][:, place], ident[:], start=(side == 0), stop=(side == 1), is_transpose=True)

        def roots(c0, w):
            for b in range(c0 // P, (c0 + w) // P):
                nc.scalar.activation(root[:, b * P : (b + 1) * P, :], banks[SUM_BANK + b][:].rearrange("p (t j) -> p j t", t=PACK), ACT.Sqrt, bias=0.05)

        for i in range(last + 2):
            if i <= last:
                c0, w, t, sides = STEPS[i]
                if sides[0] == 0:
                    gathers(c0, w, t)
                add_own_and_first(i)
                add_lift(i)
            if i < N // P:
                cols = slice(i * P, (i + 1) * P)
                nc.scalar.copy(w2_bf[:, cols, :].rearrange("p (c i) t -> p c t i", i=4), w2_raw[:, :, cols].rearrange("p t (c i) -> p c t i", i=4))
            if i >= 1:
                square_and_turn_back(i - 1)
                c0, w, t, sides = STEPS[i - 1]
                if t == LAST_TILE and sides[-1] == 1:
                    roots(c0, w)


        rise = keep.tile([P, 2, 2, P], F32, align_bytes=64, tag="neg0", name="rise")
        for side in range(2):
            for k, name in enumerate((FIRST_LISTS[side], SECOND_LISTS[side])):
                nc.vector.tensor_tensor(rise[:, k, side, :], y[LAST_TILE][:].indirect(lists[name][:, (S - P) // 16 :]), own[:], ALU.subtract)
        drop = keep.tile([P, 2, P], F32)
        nc.vector.scalar_tensor_tensor(drop[:], rise[:, 0, :, :], 0.0, rise[:, 1, :, :], ALU.min, ALU.min)
        drop_square = keep.tile([P, 2, P], F32)
        nc.vector.tensor_tensor(drop_square[:], drop[:], drop[:], ALU.mult)
        total = keep.tile([P, P], F32)
        nc.vector.tensor_tensor(total[:], drop_square[:, 0, :], drop_square[:, 1, :], ALU.add)
        last_root = keep.tile([P, PACK, P], F32, align_bytes=64, tag="square%d" % (last % RING), name="last_root")
        nc.scalar.activation(last_root[:, 0:LAST_TILE, :], banks[SUM_BANK + PACK - 1][:, 0 : LAST_TILE * P].rearrange("p (t j) -> p t j", t=LAST_TILE), ACT.Sqrt, bias=0.05)
        nc.scalar.activation(last_root[:, LAST_TILE, :], total[:], ACT.Sqrt, bias=0.05)

        w2_codes = keep.tile([P, N], U32, align_bytes=64, tag="gap2", name="w2_codes")
        w2_scales = keep.tile([P, N], U8, align_bytes=64)
        nc.vector.quantize_mx(out=w2_codes[:].bitcast(FP8X4), scales=w2_scales[:], in_=w2_bf[:].rearrange("p c t -> p (c t)"))
        z = keep.tile([P, S, PACK], BF16, align_bytes=64, tag="neg1", name="z")
        z_codes = keep.tile([P, S], U32, align_bytes=64, tag="pos%d" % (last % RING), name="z_codes")
        z_scales = keep.tile([P, S], U8, align_bytes=64)
        for c0, w, bank0 in GROUPS:
            src = root[:, c0 : c0 + w, :] if c0 + w < S else last_root[:].rearrange("p t j -> p j t")
            nc.vector.tensor_tensor(z[:, c0 : c0 + w, :], src, gain[:].unsqueeze(1).to_broadcast([P, w, PACK]), ALU.mult)
        out_v = out.rearrange("(g p) n -> p g n", p=P)
        for c0, w, bank0 in GROUPS:
            cols = slice(c0, c0 + w)
            nc.vector.quantize_mx(out=z_codes[:, cols].bitcast(FP8X4), scales=z_scales[:, cols], in_=z[:, cols, :].rearrange("p j t -> p (j t)"))
            for h in range(2):
                acc = banks[bank0 + h]
                for g in range(2):
                    rows = slice((2 * h + g) * P, (2 * h + g + 1) * P)
                    nc.tensor.matmul_mx(out=acc[:, g * w : (g + 1) * w], lhsT=w2_codes[:, rows].bitcast(FP8X4), lhsT_scale=w2_scales[:, rows], rhs=z_codes[:, cols].bitcast(FP8X4), rhs_scale=z_scales[:, cols], start=True, stop=True)
                res = keep.tile([P, 2, w], F32, name="res%d_%d" % (c0, h))
                if c0 > 0 and h == 1:
                    nc.vector.tensor_copy(res[:], acc[:, 0 : 2 * w].rearrange("p (g j) -> p g j", g=2))
                else:
                    nc.scalar.copy(res[:], acc[:, 0 : 2 * w].rearrange("p (g j) -> p g j", g=2))
                queue = nc.scalar if (c0 + w == S and h == 0) else nc.sync
                queue.dma_start(out_v[:, 2 * h : 2 * h + 2, cols], res[:])
